import numpy as np
import ml_dtypes


def mxq(x, axis, fmt="e4m3"):
    dtype, down = {"e4m3": (ml_dtypes.float8_e4m3fn, 7), "e5m2": (ml_dtypes.float8_e5m2, 14)}[fmt]
    v = np.moveaxis(np.asarray(x, np.float32).astype(ml_dtypes.bfloat16).astype(np.float64), axis, -1)
    blocks = v.reshape(v.shape[:-1] + (-1, 32))
    amax = np.abs(blocks).max(-1, keepdims=True)
    byte = np.maximum(np.where(amax > 0, np.frexp(amax)[1] - 1 + 127, 0) - down, 1)
    scale = np.exp2(byte - 127.0)
    codes = (blocks / scale).astype(np.float32).astype(dtype).astype(np.float64)
    return np.moveaxis((codes * scale).reshape(v.shape), -1, axis)


WIDE = False


def mx_kscale(k):
    if not WIDE:
        return np.ones(k)
    levels = np.array([10, -10, 5, -5, 0])
    if k % 512:
        return np.exp2(np.random.permutation(np.resize(levels, k // 32))).repeat(32)
    a = np.empty((k // 512, 16))
    for p in range(k // 512):
        a[p, :8] = np.random.permutation(np.resize(levels, 8))
        for g in range(8):
            far = levels[np.abs(levels - a[p, g]) >= 10]
            a[p, g + 8] = far[np.random.randint(len(far))]
    return np.exp2(a.ravel()).repeat(32)


def f64(x):
    return np.asarray(x).astype(np.float64)


def striped(idx):
    return np.tile(idx.reshape(-1, 16).T, (8, 1)).astype(np.uint16)


def unstriped(offs):
    return offs[:16].T.reshape(-1).astype(np.int64)


E2M1 = np.array([0.0, 0.5, 1.0, 1.5, 2.0, 3.0, 4.0, 6.0, -0.0, -0.5, -1.0, -1.5, -2.0, -3.0, -4.0, -6.0])


def pack_weight(w, fmt):
    k, n = w.shape
    w = f64(np.asarray(w, np.float32).astype(ml_dtypes.bfloat16)).reshape(k // 32, 32, n)
    amax = np.abs(w).max(1)
    if fmt == "e4m3":
        byte = np.frexp(amax)[1] - 1 + 127 - 7
    else:
        mant, ex = np.frexp(amax / 6.0)
        byte = np.where(mant > 0.5, ex, ex - 1) + 127
    byte = np.clip(np.where(amax > 0, byte, 1), 1, 254)
    scaled = (w * np.exp2(127.0 - byte)[:, None, :]).reshape(k, n).astype(np.float32)
    by_word = np.ascontiguousarray(scaled.reshape(k // 512, 128, 4, n).transpose(0, 1, 3, 2))
    if fmt == "e4m3":
        words = by_word.astype(ml_dtypes.float8_e4m3fn).view(np.uint8)
    else:
        c = by_word.astype(ml_dtypes.float4_e2m1fn).view(np.uint8) & 0xF
        words = (c[..., 0::2] | (c[..., 1::2] << 4)).reshape(k // 512, 128, 2 * n)
    return np.ascontiguousarray(words), np.ascontiguousarray(byte.astype(np.uint8).reshape(k // 512, 16, n))


def unpack_weight(words, scales, fmt):
    g, _, n = scales.shape
    words = np.ascontiguousarray(words).reshape(g, 128, n, -1)
    if fmt == "e4m3":
        vals = words.view(ml_dtypes.float8_e4m3fn).astype(np.float64)
    else:
        nib = np.empty((g, 128, n, 4), np.uint8)
        nib[..., 0::2] = words & 0xF
        nib[..., 1::2] = words >> 4
        vals = E2M1[nib]
    vals = vals * np.repeat(np.exp2(scales.astype(np.float64) - 127.0), 8, axis=1)[..., None]
    return vals.transpose(0, 1, 3, 2).reshape(g * 512, n)


def gelu(v):
    return 0.5 * v * (1.0 + np.tanh(np.sqrt(2.0 / np.pi) * (v + 0.044715 * v**3)))


K, K1, H, T, S, T2, T3, S2, P = 1024, 512, 1024, 2048, 512, 1024, 2048, 512, 512

def setup_inputs():
    n = np.random.standard_normal
    s = mx_kscale(K)[:, None]
    u = mx_kscale(H)[:, None]
    tab_words, tab_scales = pack_weight(n((K, T)) * s, "e4m3")
    tab2_words, tab2_scales = pack_weight(n((H, T3)) / np.sqrt(H) / u, "e4m3")
    w4_words, w4_scales = pack_weight(0.55 * n((K1, H)) / np.sqrt(K) / s[:K1], "e2m1")
    return {
        "tab_words": tab_words, "tab_scales": tab_scales,
        "tab2_words": tab2_words, "tab2_scales": tab2_scales,
        "w4_words": w4_words, "w4_scales": w4_scales,
        "w1": (0.55 * n((K - K1, H)) / np.sqrt(K) / s[K1:]).astype(np.float32),
        "gain": (1.6 * np.exp(0.3 * n(H)) * u[:, 0]).astype(np.float32),
        "wgs": np.exp(0.3 * n((128, S))).astype(np.float32),
        "page0": (n((H, T2)) * u).astype(np.float32),
        "wear": np.exp(0.4 * n((H, T2))).astype(np.float32),
        "shift": (0.7 * n((H, T2)) * u).astype(np.float32),
        "cv": np.exp(0.4 * n(S2)).astype(np.float32),
        "offs": striped(np.random.permutation(T)[:S]),
        "offs2": striped(np.random.permutation(T3)[:S2]),
        "offs3": striped(np.random.permutation(T2)[:S]),
        "pos1": striped(np.random.permutation(T2)[:P]),
        "pos2": striped(np.random.permutation(T2)[:P]),
    }

def reference(tab_words, tab_scales, tab2_words, tab2_scales, w4_words, w4_scales, w1, gain, wgs, page0, wear, shift, cv, offs, offs2, offs3, pos1, pos2):
    v = unpack_weight(tab_words, tab_scales, "e4m3")[:, unstriped(offs)]
    v2 = unpack_weight(tab2_words, tab2_scales, "e4m3")[:, unstriped(offs2)]
    w4 = unpack_weight(w4_words, w4_scales, "e2m1")
    w1q = mxq(f64(w1), 0, "e4m3")
    h = f64(gain)[:, None] * np.sin(w4.T @ v[:K1] + w1q.T @ v[K1:])
    page = f64(page0).copy()
    page[:, unstriped(offs3)] = np.tile(f64(wgs), (H // 128, 1)) * h
    x = mxq(page * f64(wear) + f64(shift), 0, "e4m3")
    e = v2.T @ x
    butt = e[:, unstriped(pos1)]
    top = e[:, unstriped(pos2)]
    return np.maximum(butt - top, f64(cv)[:, None] * top)

@@ -1,0 +1,412 @@
+import math
+from contextlib import ExitStack
+
+import concourse.mybir as mybir
+from concourse.masks import make_identity
+
+FLOPS = 2147483648
+
+F32 = mybir.dt.float32
+BF16 = mybir.dt.bfloat16
+I32 = mybir.dt.int32
+U32 = mybir.dt.uint32
+U16 = mybir.dt.uint16
+U8 = mybir.dt.uint8
+FP8X4 = mybir.dt.float8_e4m3fn_x4
+FP4X4 = mybir.dt.float4_e2m1fn_x4
+ALU = mybir.AluOpType
+ACT = mybir.ActivationFunctionType
+
+P = 128
+PACK = 4
+K_PASS = P * PACK
+T = 2048
+S = 512
+H = 1024
+T2 = 1024
+BANK = 512
+TWO_PI = 2.0 * math.pi
+TURN_OFFSET = 2.0**21 - 0.25
+
+
+def tile_list_veneer_log_grading_kernel(
+    tc, tab_words, tab_scales, tab2_words, tab2_scales, w4_words, w4_scales, w1, gain, wgs,
+    page0, wear, shift, cv, offs, offs2, offs3, pos1, pos2, out,
+):
+    nc = tc.nc
+    with ExitStack() as ctx:
+        keep = ctx.enter_context(tc.tile_pool(name="keep", bufs=1))
+        ring = ctx.enter_context(tc.tile_pool(name="ring", bufs=3))
+        reuse = ctx.enter_context(tc.tile_pool(name="reuse", bufs=1))
+        psum = ctx.enter_context(tc.psum_pool(name="psum", bufs=1))
+
+        def banks(pair, name):
+            return psum.tile([P, 2, BANK], F32, name=name, tag="pair%d" % pair)
+
+        def load_list(src, name):
+            tile = keep.tile([P, S // 16], U16, name=name)
+            nc.sync.dma_start(tile[:], src)
+            return tile
+
+        def load_words(src, a, tile):
+            nc.sync.dma_start(tile[:].bitcast(I32), src[a].rearrange("p t i -> p (t i)").bitcast(I32))
+            return tile
+
+        def load_scale_rows(src, tile):
+            rows = 4 * src.shape[0]
+            for q in range(4):
+                nc.sync.dma_start(
+                    tile[32 * q : 32 * q + rows, :].bitcast(I32), src[:, 4 * q : 4 * q + 4, :].bitcast(I32)
+                )
+
+        def gather(window, offsets, dtype, name, tag):
+            tile = keep.tile([P, S], dtype, name=name, tag=tag, align_bytes=64)
+            nc.vector.tensor_copy(tile[:], window[:].indirect(offsets[:]))
+            return tile
+
+        tab_s = keep.tile([P, T], U8, name="tab_s")
+        w_s = keep.tile([P, K_PASS], U8, name="w_s", align_bytes=64)
+        w4_s_hi = keep.tile([P, K_PASS], U8, name="w4_s_hi")
+        tab2_s = keep.tile([P, T], U8, name="tab2_s")
+        nc.gpsimd.memset(tab_s[:].bitcast(I32), 0)
+        nc.vector.memset(w4_s_hi[:].bitcast(I32), 0)
+        nc.vector.memset(tab2_s[:].bitcast(I32), 0)
+        ident = keep.tile([P, P], F32, name="ident")
+        make_identity(nc, ident[:])
+        one = keep.tile([P, 1], F32, name="one")
+        half_pi = keep.tile([P, 1], F32, name="half_pi")
+        nc.vector.memset(one[:], 1.0)
+        nc.vector.tensor_scalar(half_pi[:], one[:], math.pi / 2.0, None, ALU.mult)
+
+        load_scale_rows(w4_scales[:, :, 0:K_PASS], w_s)
+        idx = load_list(offs, "idx")
+        w1_rows = w1.rearrange("(p j) c -> p j c", j=PACK)
+        w1_parts = [(0, P), (P, K_PASS), (K_PASS, H)]
+        w1_raw = []
+
+        def load_w1(part):
+            c0, c1 = w1_parts[part]
+            tile = keep.tile([P, PACK, c1 - c0], F32, name="w1_raw%d" % part, align_bytes=64)
+            nc.sync.dma_start(tile[:], w1_rows[:, :, c0:c1])
+            w1_raw.append(tile)
+
+        gain_lo = keep.tile([P, PACK], F32, name="gain_lo")
+        gain_hi = keep.tile([P, PACK], F32, name="gain_hi")
+        cv_sb = keep.tile([P, PACK], F32, name="cv_sb")
+        tab_w = [load_words(tab_words, 0, keep.tile([P, T], U32, name="tab_w0", tag="words0"))]
+        load_scale_rows(tab_scales, tab_s)
+        load_w1(0)
+        w4_w = keep.tile([P, 2 * H], U8, name="w4_w", align_bytes=64)
+        nc.sync.dma_start(w4_w[:].bitcast(I32), w4_words[0].bitcast(I32))
+        tab_w.append(load_words(tab_words, 1, reuse.tile([P, T], U32, name="tab_w1", offset=2048, align_bytes=64)))
+        load_w1(1)
+        wgs_sb = keep.tile([P, S], F32, name="wgs_sb")
+        nc.sync.dma_start(wgs_sb[:], wgs)
+        with nc.allow_non_contiguous_dma(reason="one value to a partition"):
+            nc.sync.dma_start(gain_lo[:], gain[0:K_PASS].rearrange("(c p) -> p c", p=P))
+        idx3 = load_list(offs3, "idx3")
+
+        def rows_of(src, r):
+            if r < PACK:
+                return src[P * r : P * (r + 1), :]
+            return src[K_PASS:H, :].rearrange("(p t) n -> p t n", t=PACK)[:, r - PACK, :]
+
+        pages = []
+
+        def load_page(r):
+            tile = keep.tile([P, T2], F32, name="page%d" % r, align_bytes=64)
+            nc.sync.dma_start(tile[:], rows_of(page0, r))
+            pages.append(tile)
+
+        wear_lo = []
+        shift_lo = []
+
+        def load_wear(r):
+            tile = keep.tile([P, T2], F32, name="wear%d" % r, tag="wear%d" % (r % PACK))
+            wear_lo.append(tile)
+            nc.sync.dma_start(tile[:], rows_of(wear, r))
+
+        def load_shift(r):
+            tile = keep.tile([P, T2], F32, name="shift%d" % r, tag="rows%d" % r)
+            shift_lo.append(tile)
+            nc.sync.dma_start(tile[:], rows_of(shift, r))
+
+        load_page(0)
+        load_page(1)
+        load_w1(2)
+        load_scale_rows(w4_scales[:, :, K_PASS:H], w4_s_hi)
+        nc.sync.dma_start(gain_hi[:], gain[K_PASS:H].rearrange("(p t) -> p t", t=PACK))
+        load_wear(0)
+        load_page(2)
+        load_shift(0)
+        load_wear(1)
+        load_page(3)
+        load_shift(1)
+        wgs_dealt = keep.tile([P, PACK, S], F32, name="wgs_dealt")
+        for q in range(4):
+            nc.sync.dma_start(wgs_dealt[32 * q : 32 * q + 32, :, :], wgs.rearrange("(q t) j -> q t j", t=PACK))
+        load_wear(2)
+        load_page(4)
+        load_shift(2)
+        load_wear(3)
+        load_page(5)
+        load_shift(3)
+        load_page(6)
+        load_page(7)
+        idx2 = load_list(offs2, "idx2")
+        load_scale_rows(tab2_scales, tab2_s)
+
+        v_s = gather(tab_s, idx, U8, "v_s", "v_s")
+        v_w = [gather(tab_w[a], idx, U32, "v_w%d" % a, "v_w%d" % a) for a in range(2)]
+
+        tab2_w = [
+            load_words(tab2_words, a, keep.tile([P, T], U32, name="tab2_w%d" % a, tag="words%d" % a))
+            for a in range(2)
+        ]
+        with nc.allow_non_contiguous_dma(reason="one value to a partition"):
+            nc.sync.dma_start(cv_sb[:], cv.rearrange("(c p) -> p c", p=P))
+        p1 = load_list(pos1, "p1")
+        p2 = load_list(pos2, "p2")
+
+        w1_c = []
+
+        def quantise_w1(part):
+            c0, c1 = w1_parts[part]
+            width = c1 - c0
+            if part == 1:
+                grouped = reuse.tile([P, width, PACK], BF16, name="w1_bf1", offset=2048, align_bytes=64)
+            elif part == 2:
+                grouped = reuse.tile([P, width, PACK], BF16, name="w1_bf2", offset=16384 + 1536, align_bytes=64)
+            else:
+                grouped = keep.tile([P, width, PACK], BF16, name="w1_bf0", align_bytes=64)
+            raw = w1_raw[part]
+            if part < 2:
+                nc.vector.tensor_copy(
+                    grouped[:].rearrange("p (c i) j -> p c j i", i=4), raw[:].rearrange("p j (c i) -> p c j i", i=4)
+                )
+            else:
+                nc.scalar.copy(
+                    grouped[:].rearrange("p (t q) j -> p q j t", t=PACK),
+                    raw[:].rearrange("p j (q t) -> p q j t", t=PACK),
+                )
+            codes = keep.tile([P, width], U32, name="w1_c%d" % part, align_bytes=64)
+            w1_c.append(codes)
+            if part == 2:
+                cuts = [(0, width, w1_s_hi[:])]
+            elif part == 1:
+                cuts = [(0, P, w_s[4:P, P : 2 * P]), (P, width, w_s[4:P, 2 * P : K_PASS])]
+            else:
+                cuts = [(0, P, w_s[4:P, 0:P])]
+            for lo, hi, scales in cuts:
+                nc.vector.quantize_mx(
+                    out=codes[:, lo:hi].bitcast(FP8X4), scales=scales,
+                    in_=grouped[:, lo:hi, :].rearrange("p c j -> p (c j)"),
+                )
+
+        w1_s_hi = keep.tile([P, K_PASS], U8, name="w1_s_hi", align_bytes=64)
+
+        def deal_w4():
+            w4_w_dealt = reuse.tile([P, 2 * K_PASS], U8, name="w4_w_dealt", offset=16384, align_bytes=64)
+            w4_s_dealt = reuse.tile([P, K_PASS], U8, name="w4_s_dealt", offset=16384 + 1024, align_bytes=64)
+            dealt.extend([w4_w_dealt, w4_s_dealt])
+            nc.vector.tensor_copy(
+                w4_w_dealt[:].rearrange("p (t q b) -> p t q b", t=PACK, b=2),
+                w4_w[:, 2 * K_PASS : 2 * H].rearrange("p (q t b) -> p t q b", t=PACK, b=2),
+            )
+            nc.vector.tensor_copy(
+                w4_s_dealt[:].rearrange("p (t q) -> p t q", t=PACK),
+                w4_s_hi[:].rearrange("p (q t) -> p t q", t=PACK),
+            )
+
+        dealt = []
+        sines = {}
+        weights = {}
+        angles = {}
+
+        def weigh(r):
+            if r <= PACK:
+                offset = (6144, 2048, 4096, 8192, 12288)[r]
+                weight = reuse.tile([P, S], F32, name="weight%d" % r, offset=offset, align_bytes=64)
+            else:
+                tag = "worn_hi" if r == 2 * PACK - 1 else "weight%d" % r
+                weight = keep.tile([P, S], F32, name="weight%d" % r, tag=tag, align_bytes=64)
+            if r < PACK:
+                nc.vector.tensor_scalar(weight[:], wgs_sb[:], gain_lo[:, r : r + 1], None, ALU.mult)
+            else:
+                t = r - PACK
+                nc.scalar.activation(weight[:], wgs_dealt[:, t, :], ACT.Copy, scale=gain_hi[:, t : t + 1])
+            weights[r] = weight
+
+        def first_product(r):
+            if r < PACK:
+                w4_codes = w4_w[:, 2 * P * r : 2 * P * (r + 1)]
+                w4_scale = w_s[:, P * r : P * (r + 1)]
+                w1_scale = w_s[4:P, P * r : P * (r + 1)]
+                part = min(r, 1)
+                col = P * r - w1_parts[part][0]
+            else:
+                t = r - PACK
+                w4_codes = dealt[0][:, 2 * P * t : 2 * P * (t + 1)]
+                w4_scale = dealt[1][:, P * t : P * (t + 1)]
+                w1_scale = w1_s_hi[:, P * t : P * (t + 1)]
+                part = 2
+                col = P * t
+            y = banks(r % 4, "y%d" % r)[:, 0, :]
+            nc.tensor.matmul_mx(
+                y, lhsT=w4_codes.bitcast(FP4X4), lhsT_scale=w4_scale,
+                rhs=v_w[0][:].bitcast(FP8X4), rhs_scale=v_s[:], start=True, stop=False,
+            )
+            nc.tensor.matmul_mx(
+                y, lhsT=w1_c[part][:, col : col + P].bitcast(FP8X4), lhsT_scale=w1_scale,
+                rhs=v_w[1][:].bitcast(FP8X4), rhs_scale=v_s[4:P, :], start=False, stop=True,
+            )
+            turns = ring.tile([P, S], U32, name="turns", bufs=2)
+            nc.scalar.activation(turns[:], y, ACT.Copy, bias=TURN_OFFSET, scale=1.0 / TWO_PI)
+            whole = keep.tile([P, S], F32, name="whole%d" % r, tag="slot%d" % (r % 3), align_bytes=64)
+            nc.scalar.activation(whole[:], turns[:], ACT.Copy, bias=-TURN_OFFSET, scale=1.0)
+            angle = ring.tile([P, S], F32, name="angle")
+            nc.vector.scalar_tensor_tensor(angle[:], whole[:], -TWO_PI, y, ALU.mult, ALU.add)
+            angles[r] = angle
+
+        def sine_of(r):
+            angle = angles[r]
+            nc.scalar.activation(angle[:], angle[:], ACT.Abs)
+            if r == 0:
+                sine = reuse.tile([P, S], F32, name="sine0", offset=16384, align_bytes=64)
+            else:
+                tag = "slot%d" % ((r + 1) % 3) if r < 2 * PACK - 1 else "sine%d" % r
+                sine = keep.tile([P, S], F32, name="sine%d" % r, tag=tag, align_bytes=64)
+            nc.scalar.activation(sine[:], angle[:], ACT.Sin, bias=half_pi[:], scale=-1.0)
+            sines[r] = sine
+
+        def replace(r):
+            nc.vector.tensor_tensor(pages[r][:].indirect(idx3[:]), sines[r][:], weights[r][:], ALU.mult)
+
+        def apply_wear(r, dst):
+            nc.vector.tensor_tensor(dst, pages[r][:], wear_lo[r][:], ALU.mult)
+
+        x_turned = [keep.tile([P, 4, 2, P, 2], BF16, name="x_turned%d" % h) for h in range(2)]
+
+        def add_shift_turned(r):
+            product = reuse.tile([P, T2], F32, name="worn%d" % r, offset=4096 * r, align_bytes=64)
+            apply_wear(r, product[:])
+            acc = banks((r + 2) % 4, "xt%d" % r)
+            for h in range(2):
+                for which, src in enumerate((shift_lo[r], product)):
+                    for k in range(4):
+                        n0 = BANK * h + P * k
+                        nc.tensor.matmul(
+                            acc[:, h, P * k : P * (k + 1)], lhsT=src[:, n0 : n0 + P], rhs=ident[:],
+                            is_transpose=True, start=(which == 0 and k == 0), stop=(which == 1 and k == 3),
+                        )
+                nc.scalar.copy(
+                    x_turned[h][:, :, :, 32 * r : 32 * (r + 1), :],
+                    acc[:, h, :].rearrange("n (k q u e) -> n k u q e", k=4, u=2, e=2),
+                )
+
+        x_in = {}
+        x_c = {}
+        x_s = {}
+
+        def quantise_x(a, h):
+            codes = keep.tile([P, BANK], U32, name="x_c%d_%d" % (a, h), align_bytes=64)
+            scales = keep.tile([P, BANK], U8, name="x_s%d_%d" % (a, h), align_bytes=64)
+            nc.vector.quantize_mx(
+                out=codes[:].bitcast(FP8X4), scales=scales[:], in_=x_in[a, h][:].rearrange("p n t -> p (n t)")
+            )
+            x_c[a, h] = codes
+            x_s[a, h] = scales
+
+        def turn_back(h):
+            x_in[0, h] = keep.tile([P, BANK, PACK], BF16, name="x_in0_%d" % h, tag="page%d" % h, align_bytes=64)
+            words = x_turned[h][:].rearrange("n k u p e -> n (k u p e)").bitcast(F32)
+            dst = x_in[0, h][:].rearrange("p n t -> p (n t)").bitcast(F32)
+            pair = banks(h, "xw%d" % h)
+            for g in range(2):
+                acc = pair[:, g, :]
+                for i in range(4):
+                    w0 = BANK * g + P * i
+                    nc.tensor.transpose(acc[:, P * i : P * (i + 1)], words[:, w0 : w0 + P], ident[:])
+                nc.scalar.copy(
+                    dst[:, BANK * g : BANK * (g + 1)].rearrange("p (k n u) -> p k n u", k=2, u=2),
+                    acc.rearrange("p (k u n) -> p k n u", k=2, u=2),
+                )
+            quantise_x(0, h)
+
+        last = 2 * PACK - 1
+        quantise_w1(0)
+        first_product(0)
+        quantise_w1(1)
+        sine_of(0)
+        first_product(1)
+        for r in range(PACK):
+            weigh(r)
+        for r in range(last + 1):
+            if r + 2 <= last:
+                first_product(r + 2)
+            if r + 1 <= last:
+                sine_of(r + 1)
+            if PACK <= r + 1 <= last:
+                weigh(r + 1)
+            replace(r)
+            if r == 0:
+                deal_w4()
+                quantise_w1(2)
+            if 1 <= r <= PACK:
+                add_shift_turned(r - 1)
+                load_wear(PACK + r - 1)
+            if r == PACK + 1:
+                v2_s = gather(tab2_s, idx2, U8, "v2_s", "weight5")
+            if r == PACK + 2:
+                v2_w = [gather(tab2_w[0], idx2, U32, "v2_w0", "weight6"), gather(tab2_w[1], idx2, U32, "v2_w1", "slot1")]
+        shift_hi = keep.tile([P, PACK, T2], F32, name="shift_hi", tag="w1_raw2", align_bytes=64)
+        for t in range(PACK):
+            nc.sync.dma_start(shift_hi[:, t, :], rows_of(shift, PACK + t))
+        turn_back(0)
+        turn_back(1)
+        worn_hi = keep.tile([P, PACK, T2], F32, name="worn_hi", tag="worn_hi", align_bytes=64)
+        for t in range(PACK):
+            apply_wear(PACK + t, worn_hi[:, t, :])
+
+        scores = [banks(m, "e%d" % m) for m in range(4)]
+
+        def score(a, m, h):
+            nc.tensor.matmul_mx(
+                scores[m][:, h, :], lhsT=v2_w[a][:, P * m : P * (m + 1)].bitcast(FP8X4),
+                lhsT_scale=v2_s[4 * a : P, P * m : P * (m + 1)],
+                rhs=x_c[a, h][:].bitcast(FP8X4), rhs_scale=x_s[a, h][:], start=(a == 0), stop=(a == 1),
+            )
+
+        for h in range(2):
+            for m in range(4):
+                score(0, m, h)
+
+        e_sb = [keep.tile([P, T2], F32, name="e%d" % m, tag="rows%d" % m) for m in range(4)]
+        for h in range(2):
+            cols = slice(BANK * h, BANK * (h + 1))
+            x_in[1, h] = keep.tile([P, BANK, PACK], BF16, name="x_in1_%d" % h, tag="page%d" % (2 + h), align_bytes=64)
+            nc.vector.tensor_tensor(
+                x_in[1, h][:].rearrange("p (c i) t -> p c t i", i=4),
+                worn_hi[:, :, cols].rearrange("p t (c i) -> p c t i", i=4),
+                shift_hi[:, :, cols].rearrange("p t (c i) -> p c t i", i=4),
+                ALU.add,
+            )
+            quantise_x(1, h)
+            for m in range(4):
+                score(1, m, h)
+                nc.scalar.copy(e_sb[m][:, cols], scores[m][:, h, :])
+
+        halves = [(slice(256 * g, 256 * (g + 1)), slice(16 * g, 16 * (g + 1))) for g in range(2)]
+        for m in range(4):
+            top = ring.tile([P, S], F32, name="top", tag="angle")
+            diff = keep.tile([P, S], F32, name="diff%d" % m, tag="slot%d" % (m % 3), align_bytes=64)
+            best = ring.tile([P, S], F32, name="best", tag="turns", bufs=2)
+            for cols, lst in halves:
+                nc.vector.tensor_copy(top[:, cols], e_sb[m][:].indirect(p2[:, lst]))
+            for cols, lst in halves:
+                nc.vector.tensor_tensor(diff[:, cols], e_sb[m][:].indirect(p1[:, lst]), top[:, cols], ALU.subtract)
+            for cols, lst in halves:
+                nc.vector.scalar_tensor_tensor(
+                    best[:, cols], top[:, cols], cv_sb[:, m : m + 1], diff[:, cols], ALU.mult, ALU.max
+                )
+            nc.sync.dma_start(out[P * m : P * (m + 1), :], best[:])

@@ -25,8 +25,16 @@ S = 512
 H = 1024
 T2 = 1024
 BANK = 512
+ROW_TILES = H // P
+LAST = ROW_TILES - 1
 TWO_PI = 2.0 * math.pi
 TURN_OFFSET = 2.0**21 - 0.25
+WHOLE = [slice(0, S)]
+HALVES = [slice(0, S // 2), slice(S // 2, S)]
+
+
+def list_columns(cols):
+    return slice(cols.start // 16, cols.stop // 16)
 
 
 def tile_list_veneer_log_grading_kernel(
@@ -40,8 +48,8 @@ def tile_list_veneer_log_grading_kernel(
         reuse = ctx.enter_context(tc.tile_pool(name="reuse", bufs=1))
         psum = ctx.enter_context(tc.psum_pool(name="psum", bufs=1))
 
-        def banks(pair, name):
-            return psum.tile([P, 2, BANK], F32, name=name, tag="pair%d" % pair)
+        def bank(b, name):
+            return psum.tile([P, BANK], F32, name=name, tag="bank%d" % b)
 
         def load_list(src, name):
             tile = keep.tile([P, S // 16], U16, name=name)
@@ -52,24 +60,23 @@ def tile_list_veneer_log_grading_kernel(
             nc.sync.dma_start(tile[:].bitcast(I32), src[a].rearrange("p t i -> p (t i)").bitcast(I32))
             return tile
 
-        def load_scale_rows(src, tile):
+        def load_scale_rows(src, tile, queue):
             rows = 4 * src.shape[0]
             for q in range(4):
-                nc.sync.dma_start(
+                queue.dma_start(
                     tile[32 * q : 32 * q + rows, :].bitcast(I32), src[:, 4 * q : 4 * q + 4, :].bitcast(I32)
                 )
 
-        def gather(window, offsets, dtype, name, tag):
-            tile = keep.tile([P, S], dtype, name=name, tag=tag, align_bytes=64)
-            nc.vector.tensor_copy(tile[:], window[:].indirect(offsets[:]))
+        def gather(tile, window, offsets, pieces):
+            for cols in pieces:
+                nc.vector.tensor_copy(tile[:, cols], window[:].indirect(offsets[:, list_columns(cols)]))
             return tile
 
         tab_s = keep.tile([P, T], U8, name="tab_s")
-        w_s = keep.tile([P, K_PASS], U8, name="w_s", align_bytes=64)
-        w4_s_hi = keep.tile([P, K_PASS], U8, name="w4_s_hi")
+        w_s = keep.tile([P, H], U8, name="w_s", align_bytes=64)
         tab2_s = keep.tile([P, T], U8, name="tab2_s")
         nc.gpsimd.memset(tab_s[:].bitcast(I32), 0)
-        nc.vector.memset(w4_s_hi[:].bitcast(I32), 0)
+        load_scale_rows(tab_scales, tab_s, nc.sync)
         nc.vector.memset(tab2_s[:].bitcast(I32), 0)
         ident = keep.tile([P, P], F32, name="ident")
         make_identity(nc, ident[:])
@@ -77,335 +84,295 @@ def tile_list_veneer_log_grading_kernel(
         half_pi = keep.tile([P, 1], F32, name="half_pi")
         nc.vector.memset(one[:], 1.0)
         nc.vector.tensor_scalar(half_pi[:], one[:], math.pi / 2.0, None, ALU.mult)
+        warm = keep.tile([P, 1], F32, name="warm")
+        nc.scalar.activation(warm[:], one[:], ACT.Sin)
 
-        load_scale_rows(w4_scales[:, :, 0:K_PASS], w_s)
-        idx = load_list(offs, "idx")
         w1_rows = w1.rearrange("(p j) c -> p j c", j=PACK)
         w1_parts = [(0, P), (P, K_PASS), (K_PASS, H)]
         w1_raw = []
 
         def load_w1(part):
             c0, c1 = w1_parts[part]
-            tile = keep.tile([P, PACK, c1 - c0], F32, name="w1_raw%d" % part, align_bytes=64)
+            tile = keep.tile([P, PACK, c1 - c0], F32, name="w1_raw%d" % part)
             nc.sync.dma_start(tile[:], w1_rows[:, :, c0:c1])
             w1_raw.append(tile)
 
-        gain_lo = keep.tile([P, PACK], F32, name="gain_lo")
-        gain_hi = keep.tile([P, PACK], F32, name="gain_hi")
-        cv_sb = keep.tile([P, PACK], F32, name="cv_sb")
-        tab_w = [load_words(tab_words, 0, keep.tile([P, T], U32, name="tab_w0", tag="words0"))]
-        load_scale_rows(tab_scales, tab_s)
+        def load_rows(src, r, tag):
+            tile = keep.tile([P, T2], F32, name="%s_%d" % (tag, r), tag=tag, align_bytes=64)
+            nc.sync.dma_start(tile[:], src[P * r : P * (r + 1), :])
+            return tile
+
+        idx = load_list(offs, "idx")
+        tab_w = [
+            load_words(tab_words, 0, keep.tile([P, T], U32, name="tab_w0", tag="words0")),
+            load_words(tab_words, 1, reuse.tile([P, T], U32, name="tab_w1", offset=0, align_bytes=64)),
+        ]
+        load_scale_rows(w4_scales, w_s, nc.sync)
         load_w1(0)
         w4_w = keep.tile([P, 2 * H], U8, name="w4_w", align_bytes=64)
         nc.sync.dma_start(w4_w[:].bitcast(I32), w4_words[0].bitcast(I32))
-        tab_w.append(load_words(tab_words, 1, reuse.tile([P, T], U32, name="tab_w1", offset=2048, align_bytes=64)))
         load_w1(1)
         wgs_sb = keep.tile([P, S], F32, name="wgs_sb")
         nc.sync.dma_start(wgs_sb[:], wgs)
+        gain_sb = keep.tile([P, ROW_TILES], F32, name="gain_sb")
         with nc.allow_non_contiguous_dma(reason="one value to a partition"):
-            nc.sync.dma_start(gain_lo[:], gain[0:K_PASS].rearrange("(c p) -> p c", p=P))
+            nc.sync.dma_start(gain_sb[:, 0:PACK], gain[0:K_PASS].rearrange("(c p) -> p c", p=P))
         idx3 = load_list(offs3, "idx3")
 
-        def rows_of(src, r):
-            if r < PACK:
-                return src[P * r : P * (r + 1), :]
-            return src[K_PASS:H, :].rearrange("(p t) n -> p t n", t=PACK)[:, r - PACK, :]
-
-        pages = []
+        pages = {}
+        wears = {}
+        shifts = {}
 
         def load_page(r):
-            tile = keep.tile([P, T2], F32, name="page%d" % r, align_bytes=64)
-            nc.sync.dma_start(tile[:], rows_of(page0, r))
-            pages.append(tile)
-
-        wear_lo = []
-        shift_lo = []
+            pages[r] = load_rows(page0, r, "page%d" % r)
 
         def load_wear(r):
-            tile = keep.tile([P, T2], F32, name="wear%d" % r, tag="wear%d" % (r % PACK))
-            wear_lo.append(tile)
-            nc.sync.dma_start(tile[:], rows_of(wear, r))
+            wears[r] = load_rows(wear, r, "wear%d" % r)
 
         def load_shift(r):
-            tile = keep.tile([P, T2], F32, name="shift%d" % r, tag="rows%d" % r)
-            shift_lo.append(tile)
-            nc.sync.dma_start(tile[:], rows_of(shift, r))
+            shifts[r] = load_rows(shift, r, "rows%d" % (r % 6))
 
         load_page(0)
         load_page(1)
         load_w1(2)
-        load_scale_rows(w4_scales[:, :, K_PASS:H], w4_s_hi)
-        nc.sync.dma_start(gain_hi[:], gain[K_PASS:H].rearrange("(p t) -> p t", t=PACK))
-        load_wear(0)
-        load_page(2)
-        load_shift(0)
-        load_wear(1)
-        load_page(3)
-        load_shift(1)
-        wgs_dealt = keep.tile([P, PACK, S], F32, name="wgs_dealt")
-        for q in range(4):
-            nc.sync.dma_start(wgs_dealt[32 * q : 32 * q + 32, :, :], wgs.rearrange("(q t) j -> q t j", t=PACK))
-        load_wear(2)
-        load_page(4)
-        load_shift(2)
-        load_wear(3)
-        load_page(5)
-        load_shift(3)
-        load_page(6)
-        load_page(7)
-        idx2 = load_list(offs2, "idx2")
-        load_scale_rows(tab2_scales, tab2_s)
-
-        v_s = gather(tab_s, idx, U8, "v_s", "v_s")
-        v_w = [gather(tab_w[a], idx, U32, "v_w%d" % a, "v_w%d" % a) for a in range(2)]
-
-        tab2_w = [
-            load_words(tab2_words, a, keep.tile([P, T], U32, name="tab2_w%d" % a, tag="words%d" % a))
-            for a in range(2)
-        ]
+        gain_hi = keep.tile([P, PACK], F32, name="gain_hi")
         with nc.allow_non_contiguous_dma(reason="one value to a partition"):
-            nc.sync.dma_start(cv_sb[:], cv.rearrange("(c p) -> p c", p=P))
-        p1 = load_list(pos1, "p1")
-        p2 = load_list(pos2, "p2")
+            nc.sync.dma_start(gain_hi[:], gain[K_PASS:H].rearrange("(c p) -> p c", p=P))
+        for r in range(6):
+            load_wear(r)
+            load_page(r + 2)
+            load_shift(r)
+        load_wear(LAST - 1)
+        load_wear(LAST)
 
-        w1_c = []
+        v_s = gather(keep.tile([P, S], U8, name="v_s", align_bytes=64), tab_s, idx, WHOLE)
+        v_w = [
+            gather(keep.tile([P, S], U32, name="v_w0", align_bytes=64), tab_w[0], idx, WHOLE),
+            gather(keep.tile([P, S], U32, name="v_w1", align_bytes=64), tab_w[1], idx, HALVES),
+        ]
+
+        w1_c = keep.tile([P, H], U32, name="w1_c", align_bytes=64)
 
         def quantise_w1(part):
             c0, c1 = w1_parts[part]
             width = c1 - c0
-            if part == 1:
-                grouped = reuse.tile([P, width, PACK], BF16, name="w1_bf1", offset=2048, align_bytes=64)
-            elif part == 2:
-                grouped = reuse.tile([P, width, PACK], BF16, name="w1_bf2", offset=16384 + 1536, align_bytes=64)
-            else:
+            if part == 0:
                 grouped = keep.tile([P, width, PACK], BF16, name="w1_bf0", align_bytes=64)
-            raw = w1_raw[part]
-            if part < 2:
-                nc.vector.tensor_copy(
-                    grouped[:].rearrange("p (c i) j -> p c j i", i=4), raw[:].rearrange("p j (c i) -> p c j i", i=4)
-                )
             else:
-                nc.scalar.copy(
-                    grouped[:].rearrange("p (t q) j -> p q j t", t=PACK),
-                    raw[:].rearrange("p j (q t) -> p q j t", t=PACK),
-                )
-            codes = keep.tile([P, width], U32, name="w1_c%d" % part, align_bytes=64)
-            w1_c.append(codes)
-            if part == 2:
-                cuts = [(0, width, w1_s_hi[:])]
-            elif part == 1:
-                cuts = [(0, P, w_s[4:P, P : 2 * P]), (P, width, w_s[4:P, 2 * P : K_PASS])]
+                offset = 0 if part == 1 else 8192
+                grouped = reuse.tile([P, width, PACK], BF16, name="w1_bf%d" % part, offset=offset, align_bytes=64)
+            dst = grouped[:].rearrange("p (c i) j -> p c j i", i=4)
+            src = w1_raw[part][:].rearrange("p j (c i) -> p c j i", i=4)
+            if part == 1:
+                nc.vector.tensor_copy(dst, src)
             else:
-                cuts = [(0, P, w_s[4:P, 0:P])]
-            for lo, hi, scales in cuts:
+                nc.scalar.copy(dst, src)
+            cuts = [(c0, 2 * P), (2 * P, c1)] if part == 1 else [(c0, c1)]
+            for lo, hi in cuts:
                 nc.vector.quantize_mx(
-                    out=codes[:, lo:hi].bitcast(FP8X4), scales=scales,
-                    in_=grouped[:, lo:hi, :].rearrange("p c j -> p (c j)"),
+                    out=w1_c[:, lo:hi].bitcast(FP8X4), scales=w_s[4:P, lo:hi],
+                    in_=grouped[:, lo - c0 : hi - c0, :].rearrange("p c j -> p (c j)"),
                 )
 
-        w1_s_hi = keep.tile([P, K_PASS], U8, name="w1_s_hi", align_bytes=64)
-
-        def deal_w4():
-            w4_w_dealt = reuse.tile([P, 2 * K_PASS], U8, name="w4_w_dealt", offset=16384, align_bytes=64)
-            w4_s_dealt = reuse.tile([P, K_PASS], U8, name="w4_s_dealt", offset=16384 + 1024, align_bytes=64)
-            dealt.extend([w4_w_dealt, w4_s_dealt])
-            nc.vector.tensor_copy(
-                w4_w_dealt[:].rearrange("p (t q b) -> p t q b", t=PACK, b=2),
-                w4_w[:, 2 * K_PASS : 2 * H].rearrange("p (q t b) -> p t q b", t=PACK, b=2),
-            )
-            nc.vector.tensor_copy(
-                w4_s_dealt[:].rearrange("p (t q) -> p t q", t=PACK),
-                w4_s_hi[:].rearrange("p (q t) -> p t q", t=PACK),
-            )
-
-        dealt = []
         sines = {}
         weights = {}
         angles = {}
+        placed = {}
+
+        def pieces_of(r):
+            return HALVES if r == 0 else WHOLE
+
+        def region(r, shape, dtype, name):
+            return keep.tile(shape, dtype, name=name, tag="region%d" % (r % 6))
 
         def weigh(r):
-            if r <= PACK:
-                offset = (6144, 2048, 4096, 8192, 12288)[r]
-                weight = reuse.tile([P, S], F32, name="weight%d" % r, offset=offset, align_bytes=64)
+            gain_col = gain_sb[:, r : r + 1] if r < PACK else gain_hi[:, r - PACK : r - PACK + 1]
+            if r == 0:
+                weight = reuse.tile([P, S], F32, name="weight0", offset=4096, align_bytes=64)
+                nc.vector.tensor_scalar(weight[:], wgs_sb[:], gain_col, None, ALU.mult)
             else:
-                tag = "worn_hi" if r == 2 * PACK - 1 else "weight%d" % r
-                weight = keep.tile([P, S], F32, name="weight%d" % r, tag=tag, align_bytes=64)
-            if r < PACK:
-                nc.vector.tensor_scalar(weight[:], wgs_sb[:], gain_lo[:, r : r + 1], None, ALU.mult)
-            else:
-                t = r - PACK
-                nc.scalar.activation(weight[:], wgs_dealt[:, t, :], ACT.Copy, scale=gain_hi[:, t : t + 1])
+                weight = region(r - 1, [P, S], F32, "weight%d" % r)
+                nc.gpsimd.tensor_scalar(weight[:], wgs_sb[:], gain_col, 0.0, ALU.mult, ALU.add)
             weights[r] = weight
 
         def first_product(r):
-            if r < PACK:
-                w4_codes = w4_w[:, 2 * P * r : 2 * P * (r + 1)]
-                w4_scale = w_s[:, P * r : P * (r + 1)]
-                w1_scale = w_s[4:P, P * r : P * (r + 1)]
-                part = min(r, 1)
-                col = P * r - w1_parts[part][0]
-            else:
-                t = r - PACK
-                w4_codes = dealt[0][:, 2 * P * t : 2 * P * (t + 1)]
-                w4_scale = dealt[1][:, P * t : P * (t + 1)]
-                w1_scale = w1_s_hi[:, P * t : P * (t + 1)]
-                part = 2
-                col = P * t
-            y = banks(r % 4, "y%d" % r)[:, 0, :]
-            nc.tensor.matmul_mx(
-                y, lhsT=w4_codes.bitcast(FP4X4), lhsT_scale=w4_scale,
-                rhs=v_w[0][:].bitcast(FP8X4), rhs_scale=v_s[:], start=True, stop=False,
-            )
-            nc.tensor.matmul_mx(
-                y, lhsT=w1_c[part][:, col : col + P].bitcast(FP8X4), lhsT_scale=w1_scale,
-                rhs=v_w[1][:].bitcast(FP8X4), rhs_scale=v_s[4:P, :], start=False, stop=True,
-            )
-            turns = ring.tile([P, S], U32, name="turns", bufs=2)
-            nc.scalar.activation(turns[:], y, ACT.Copy, bias=TURN_OFFSET, scale=1.0 / TWO_PI)
-            whole = keep.tile([P, S], F32, name="whole%d" % r, tag="slot%d" % (r % 3), align_bytes=64)
-            nc.scalar.activation(whole[:], turns[:], ACT.Copy, bias=-TURN_OFFSET, scale=1.0)
+            rows = slice(P * r, P * (r + 1))
+            turns = region(r, [P, S], U32, "turns%d" % r)
+            whole = ring.tile([P, S], F32, name="whole", bufs=2)
             angle = ring.tile([P, S], F32, name="angle")
-            nc.vector.scalar_tensor_tensor(angle[:], whole[:], -TWO_PI, y, ALU.mult, ALU.add)
+            for i, cols in enumerate(pieces_of(r)):
+                y = bank(r % 2 + 6 * i, "y%d_%d" % (r, i))[:, 0 : cols.stop - cols.start]
+                nc.tensor.matmul_mx(
+                    y, lhsT=w4_w[:, 2 * P * r : 2 * P * (r + 1)].bitcast(FP4X4), lhsT_scale=w_s[:, rows],
+                    rhs=v_w[0][:, cols].bitcast(FP8X4), rhs_scale=v_s[:, cols], start=True, stop=False,
+                )
+                nc.tensor.matmul_mx(
+                    y, lhsT=w1_c[:, rows].bitcast(FP8X4), lhsT_scale=w_s[4:P, rows],
+                    rhs=v_w[1][:, cols].bitcast(FP8X4), rhs_scale=v_s[4:P, cols], start=False, stop=True,
+                )
+                nc.scalar.activation(turns[:, cols], y, ACT.Copy, bias=TURN_OFFSET, scale=1.0 / TWO_PI)
+                nc.scalar.activation(whole[:, cols], turns[:, cols], ACT.Copy, bias=-TURN_OFFSET, scale=1.0)
+                nc.vector.scalar_tensor_tensor(angle[:, cols], whole[:, cols], -TWO_PI, y, ALU.mult, ALU.add)
             angles[r] = angle
 
         def sine_of(r):
             angle = angles[r]
-            nc.scalar.activation(angle[:], angle[:], ACT.Abs)
             if r == 0:
-                sine = reuse.tile([P, S], F32, name="sine0", offset=16384, align_bytes=64)
+                sine = reuse.tile([P, S], F32, name="sine0", offset=8192, align_bytes=64)
             else:
-                tag = "slot%d" % ((r + 1) % 3) if r < 2 * PACK - 1 else "sine%d" % r
-                sine = keep.tile([P, S], F32, name="sine%d" % r, tag=tag, align_bytes=64)
-            nc.scalar.activation(sine[:], angle[:], ACT.Sin, bias=half_pi[:], scale=-1.0)
+                sine = ring.tile([P, S], F32, name="sine", bufs=2)
+            for cols in pieces_of(r):
+                nc.scalar.activation(angle[:, cols], angle[:, cols], ACT.Abs)
+                nc.scalar.activation(sine[:, cols], angle[:, cols], ACT.Sin, bias=half_pi[:], scale=-1.0)
             sines[r] = sine
 
+        def multiply(r):
+            placed[r] = ring.tile([P, S], F32, name="placed", bufs=2)
+            nc.gpsimd.tensor_tensor(placed[r][:], sines[r][:], weights[r][:], ALU.mult)
+
         def replace(r):
-            nc.vector.tensor_tensor(pages[r][:].indirect(idx3[:]), sines[r][:], weights[r][:], ALU.mult)
+            for cols in pieces_of(r):
+                window = pages[r][:].indirect(idx3[:, list_columns(cols)])
+                if r == 0:
+                    nc.vector.tensor_tensor(window, sines[r][:, cols], weights[r][:, cols], ALU.mult)
+                else:
+                    nc.vector.tensor_copy(window, placed[r][:, cols])
 
-        def apply_wear(r, dst):
-            nc.vector.tensor_tensor(dst, pages[r][:], wear_lo[r][:], ALU.mult)
+        x_turned = {}
+        for a in range(2):
+            for h in range(2):
+                x_turned[a, h] = keep.tile([P, 4, 2, P, 2], BF16, name="x_turned%d_%d" % (a, h))
 
-        x_turned = [keep.tile([P, 4, 2, P, 2], BF16, name="x_turned%d" % h) for h in range(2)]
+        worns = {}
+
+        def apply_wear(r):
+            worns[r] = region(r, [P, T2], F32, "worn%d" % r)
+            if r < LAST:
+                nc.gpsimd.tensor_tensor(worns[r][:], pages[r][:], wears[r][:], ALU.mult)
+            else:
+                for h in range(2):
+                    cols = slice(BANK * h, BANK * (h + 1))
+                    nc.vector.tensor_tensor(worns[r][:, cols], pages[r][:, cols], wears[r][:, cols], ALU.mult)
 
         def add_shift_turned(r):
-            product = reuse.tile([P, T2], F32, name="worn%d" % r, offset=4096 * r, align_bytes=64)
-            apply_wear(r, product[:])
-            acc = banks((r + 2) % 4, "xt%d" % r)
+            worn = worns[r]
+            c = r % PACK
             for h in range(2):
-                for which, src in enumerate((shift_lo[r], product)):
+                acc = bank(2 + 2 * (r % 2) + h, "xt%d_%d" % (r, h))
+                for which, src in enumerate((shifts[r], worn)):
                     for k in range(4):
                         n0 = BANK * h + P * k
                         nc.tensor.matmul(
-                            acc[:, h, P * k : P * (k + 1)], lhsT=src[:, n0 : n0 + P], rhs=ident[:],
+                            acc[:, P * k : P * (k + 1)], lhsT=src[:, n0 : n0 + P], rhs=ident[:],
                             is_transpose=True, start=(which == 0 and k == 0), stop=(which == 1 and k == 3),
                         )
                 nc.scalar.copy(
-                    x_turned[h][:, :, :, 32 * r : 32 * (r + 1), :],
-                    acc[:, h, :].rearrange("n (k q u e) -> n k u q e", k=4, u=2, e=2),
+                    x_turned[r // PACK, h][:, :, :, 32 * c : 32 * (c + 1), :],
+                    acc[:].rearrange("n (k q u e) -> n k u q e", k=4, u=2, e=2),
                 )
 
-        x_in = {}
         x_c = {}
         x_s = {}
 
-        def quantise_x(a, h):
+        def turn_back(a, h, banks):
+            x_in = keep.tile([P, BANK * PACK], BF16, name="x_in%d_%d" % (a, h), tag="page%d" % (2 * a + h), align_bytes=64)
             codes = keep.tile([P, BANK], U32, name="x_c%d_%d" % (a, h), align_bytes=64)
             scales = keep.tile([P, BANK], U8, name="x_s%d_%d" % (a, h), align_bytes=64)
-            nc.vector.quantize_mx(
-                out=codes[:].bitcast(FP8X4), scales=scales[:], in_=x_in[a, h][:].rearrange("p n t -> p (n t)")
-            )
-            x_c[a, h] = codes
-            x_s[a, h] = scales
-
-        def turn_back(h):
-            x_in[0, h] = keep.tile([P, BANK, PACK], BF16, name="x_in0_%d" % h, tag="page%d" % h, align_bytes=64)
-            words = x_turned[h][:].rearrange("n k u p e -> n (k u p e)").bitcast(F32)
-            dst = x_in[0, h][:].rearrange("p n t -> p (n t)").bitcast(F32)
-            pair = banks(h, "xw%d" % h)
+            words = x_turned[a, h][:].rearrange("n k u p e -> n (k u p e)").bitcast(F32)
+            dst = x_in[:].bitcast(F32)
             for g in range(2):
-                acc = pair[:, g, :]
+                acc = bank(banks[g], "xw%d_%d_%d" % (a, h, g))
                 for i in range(4):
                     w0 = BANK * g + P * i
                     nc.tensor.transpose(acc[:, P * i : P * (i + 1)], words[:, w0 : w0 + P], ident[:])
                 nc.scalar.copy(
                     dst[:, BANK * g : BANK * (g + 1)].rearrange("p (k n u) -> p k n u", k=2, u=2),
-                    acc.rearrange("p (k u n) -> p k n u", k=2, u=2),
+                    acc[:].rearrange("p (k u n) -> p k n u", k=2, u=2),
                 )
-            quantise_x(0, h)
+                if a == 1:
+                    cols = HALVES[g]
+                    nc.vector.quantize_mx(
+                        out=codes[:, cols].bitcast(FP8X4), scales=scales[:, cols],
+                        in_=x_in[:, PACK * cols.start : PACK * cols.stop],
+                    )
+            if a == 0:
+                nc.vector.quantize_mx(out=codes[:].bitcast(FP8X4), scales=scales[:], in_=x_in[:])
+            x_c[a, h] = codes
+            x_s[a, h] = scales
 
-        last = 2 * PACK - 1
         quantise_w1(0)
         first_product(0)
         quantise_w1(1)
+        weigh(0)
         sine_of(0)
         first_product(1)
-        for r in range(PACK):
-            weigh(r)
-        for r in range(last + 1):
-            if r + 2 <= last:
-                first_product(r + 2)
-            if r + 1 <= last:
-                sine_of(r + 1)
-            if PACK <= r + 1 <= last:
+        for r in range(ROW_TILES):
+            if r + 1 <= LAST:
                 weigh(r + 1)
+            if r + 2 <= LAST:
+                first_product(r + 2)
+            if r + 1 <= LAST:
+                sine_of(r + 1)
+                multiply(r + 1)
             replace(r)
+
             if r == 0:
-                deal_w4()
                 quantise_w1(2)
-            if 1 <= r <= PACK:
-                add_shift_turned(r - 1)
-                load_wear(PACK + r - 1)
+            if r >= 1:
+                apply_wear(r - 1)
+            if r >= 2:
+                add_shift_turned(r - 2)
+            if r in (2, 3):
+                load_shift(LAST - 3 + r)
+            if r == 2:
+                idx2 = load_list(offs2, "idx2")
+                load_scale_rows(tab2_scales, tab2_s, nc.sync)
+                tab2_w = [
+                    load_words(tab2_words, a, keep.tile([P, T], U32, name="tab2_w%d" % a, tag="words%d" % a))
+                    for a in range(2)
+                ]
+                cv_sb = keep.tile([P, PACK], F32, name="cv_sb")
+                with nc.allow_non_contiguous_dma(reason="one value to a partition"):
+                    nc.sync.dma_start(cv_sb[:], cv.rearrange("(c p) -> p c", p=P))
+                p1 = load_list(pos1, "p1")
+                p2 = load_list(pos2, "p2")
             if r == PACK + 1:
-                v2_s = gather(tab2_s, idx2, U8, "v2_s", "weight5")
-            if r == PACK + 2:
-                v2_w = [gather(tab2_w[0], idx2, U32, "v2_w0", "weight6"), gather(tab2_w[1], idx2, U32, "v2_w1", "slot1")]
-        shift_hi = keep.tile([P, PACK, T2], F32, name="shift_hi", tag="w1_raw2", align_bytes=64)
-        for t in range(PACK):
-            nc.sync.dma_start(shift_hi[:, t, :], rows_of(shift, PACK + t))
-        turn_back(0)
-        turn_back(1)
-        worn_hi = keep.tile([P, PACK, T2], F32, name="worn_hi", tag="worn_hi", align_bytes=64)
-        for t in range(PACK):
-            apply_wear(PACK + t, worn_hi[:, t, :])
+                turn_back(0, 0, (6, 7))
+                turn_back(0, 1, (6, 7))
+        add_shift_turned(LAST - 1)
+        apply_wear(LAST)
+        add_shift_turned(LAST)
+        v2_s = gather(keep.tile([P, S], U8, name="v2_s", tag="wear%d" % LAST, align_bytes=64), tab2_s, idx2, WHOLE)
+        v2_w = keep.tile([P, 2, S], U32, name="v2_w", tag="page%d" % LAST, align_bytes=64)
+        for a in range(2):
+            nc.vector.tensor_copy(v2_w[:, a, :], tab2_w[a][:].indirect(idx2[:]))
+        turn_back(1, 0, (0, 1))
+        turn_back(1, 1, (6, 7))
 
-        scores = [banks(m, "e%d" % m) for m in range(4)]
+        score_banks = ((0, 6), (1, 7), (0, 6), (1, 7))
+        e_sb = [keep.tile([P, T2], F32, name="e%d" % m, tag="rows%d" % (2 + m), align_bytes=64) for m in range(4)]
+        for m in range(4):
+            grades = slice(P * m, P * (m + 1))
+            for h in range(2):
+                acc = bank(score_banks[m][h], "e%d_%d" % (m, h))
+                for a, cols in ((0, WHOLE[0]), (1, HALVES[0]), (1, HALVES[1])):
+                    nc.tensor.matmul_mx(
+                        acc[:, cols], lhsT=v2_w[:, a, grades].bitcast(FP8X4), lhsT_scale=v2_s[4 * a : P, grades],
+                        rhs=x_c[a, h][:, cols].bitcast(FP8X4), rhs_scale=x_s[a, h][:, cols],
+                        start=(a == 0), stop=(cols.stop == S and a == 1),
+                    )
+                nc.scalar.copy(e_sb[m][:, BANK * h : BANK * (h + 1)], acc[:])
 
-        def score(a, m, h):
-            nc.tensor.matmul_mx(
-                scores[m][:, h, :], lhsT=v2_w[a][:, P * m : P * (m + 1)].bitcast(FP8X4),
-                lhsT_scale=v2_s[4 * a : P, P * m : P * (m + 1)],
-                rhs=x_c[a, h][:].bitcast(FP8X4), rhs_scale=x_s[a, h][:], start=(a == 0), stop=(a == 1),
-            )
 
-        for h in range(2):
-            for m in range(4):
-                score(0, m, h)
-
-        e_sb = [keep.tile([P, T2], F32, name="e%d" % m, tag="rows%d" % m) for m in range(4)]
-        for h in range(2):
-            cols = slice(BANK * h, BANK * (h + 1))
-            x_in[1, h] = keep.tile([P, BANK, PACK], BF16, name="x_in1_%d" % h, tag="page%d" % (2 + h), align_bytes=64)
-            nc.vector.tensor_tensor(
-                x_in[1, h][:].rearrange("p (c i) t -> p c t i", i=4),
-                worn_hi[:, :, cols].rearrange("p t (c i) -> p c t i", i=4),
-                shift_hi[:, :, cols].rearrange("p t (c i) -> p c t i", i=4),
-                ALU.add,
-            )
-            quantise_x(1, h)
-            for m in range(4):
-                score(1, m, h)
-                nc.scalar.copy(e_sb[m][:, cols], scores[m][:, h, :])
-
-        halves = [(slice(256 * g, 256 * (g + 1)), slice(16 * g, 16 * (g + 1))) for g in range(2)]
         for m in range(4):
             top = ring.tile([P, S], F32, name="top", tag="angle")
-            diff = keep.tile([P, S], F32, name="diff%d" % m, tag="slot%d" % (m % 3), align_bytes=64)
-            best = ring.tile([P, S], F32, name="best", tag="turns", bufs=2)
-            for cols, lst in halves:
-                nc.vector.tensor_copy(top[:, cols], e_sb[m][:].indirect(p2[:, lst]))
-            for cols, lst in halves:
-                nc.vector.tensor_tensor(diff[:, cols], e_sb[m][:].indirect(p1[:, lst]), top[:, cols], ALU.subtract)
-            for cols, lst in halves:
+            diff = ring.tile([P, S], F32, name="diff", tag="whole", bufs=2)
+            best = region(m, [P, S], F32, "best%d" % m)
+            gather(top, e_sb[m], p2, HALVES)
+            for cols in HALVES:
+                picked = e_sb[m][:].indirect(p1[:, list_columns(cols)])
+                nc.vector.tensor_tensor(diff[:, cols], picked, top[:, cols], ALU.subtract)
+            for cols in HALVES:
                 nc.vector.scalar_tensor_tensor(
                     best[:, cols], top[:, cols], cv_sb[:, m : m + 1], diff[:, cols], ALU.mult, ALU.max
                 )

@@ -158,9 +158,10 @@ def tile_list_veneer_log_grading_kernel(
             width = c1 - c0
             if part == 0:
                 grouped = keep.tile([P, width, PACK], BF16, name="w1_bf0", align_bytes=64)
+            elif part == 1:
+                grouped = reuse.tile([P, width, PACK], BF16, name="w1_bf1", offset=0, align_bytes=64)
             else:
-                offset = 0 if part == 1 else 8192
-                grouped = reuse.tile([P, width, PACK], BF16, name="w1_bf%d" % part, offset=offset, align_bytes=64)
+                grouped = reuse.tile([P, width, PACK], BF16, name="w1_bf2", offset=5120, align_bytes=64)
             dst = grouped[:].rearrange("p (c i) j -> p c j i", i=4)
             src = w1_raw[part][:].rearrange("p j (c i) -> p c j i", i=4)
             if part == 1:
@@ -183,22 +184,16 @@ def tile_list_veneer_log_grading_kernel(
             return HALVES if r == 0 else WHOLE
 
         def region(r, shape, dtype, name):
-            return keep.tile(shape, dtype, name=name, tag="region%d" % (r % 6))
+            return keep.tile(shape, dtype, name=name, tag="region%d" % (r % 6), align_bytes=64)
 
         def weigh(r):
             gain_col = gain_sb[:, r : r + 1] if r < PACK else gain_hi[:, r - PACK : r - PACK + 1]
-            if r == 0:
-                weight = reuse.tile([P, S], F32, name="weight0", offset=4096, align_bytes=64)
-                nc.vector.tensor_scalar(weight[:], wgs_sb[:], gain_col, None, ALU.mult)
-            else:
-                weight = region(r - 1, [P, S], F32, "weight%d" % r)
-                nc.gpsimd.tensor_scalar(weight[:], wgs_sb[:], gain_col, 0.0, ALU.mult, ALU.add)
-            weights[r] = weight
+            nc.gpsimd.tensor_scalar(weights[r], wgs_sb[:], gain_col, 0.0, ALU.mult, ALU.add)
 
         def first_product(r):
             rows = slice(P * r, P * (r + 1))
             turns = region(r, [P, S], U32, "turns%d" % r)
-            whole = ring.tile([P, S], F32, name="whole", bufs=2)
+            whole = keep.tile([P, S], F32, name="whole%d" % r, tag="whole%d" % (r % 2))
             angle = ring.tile([P, S], F32, name="angle")
             for i, cols in enumerate(pieces_of(r)):
                 y = bank(r % 2 + 6 * i, "y%d_%d" % (r, i))[:, 0 : cols.stop - cols.start]
@@ -217,26 +212,28 @@ def tile_list_veneer_log_grading_kernel(
 
         def sine_of(r):
             angle = angles[r]
-            if r == 0:
-                sine = reuse.tile([P, S], F32, name="sine0", offset=8192, align_bytes=64)
-            else:
-                sine = ring.tile([P, S], F32, name="sine", bufs=2)
+            sine = region(r - 1, [P, S], F32, "sine%d" % r)
             for cols in pieces_of(r):
                 nc.scalar.activation(angle[:, cols], angle[:, cols], ACT.Abs)
                 nc.scalar.activation(sine[:, cols], angle[:, cols], ACT.Sin, bias=half_pi[:], scale=-1.0)
             sines[r] = sine
 
         def multiply(r):
-            placed[r] = ring.tile([P, S], F32, name="placed", bufs=2)
-            nc.gpsimd.tensor_tensor(placed[r][:], sines[r][:], weights[r][:], ALU.mult)
+            placed[r] = []
+            for i, cols in enumerate(pieces_of(r)):
+                shape = [P, cols.stop - cols.start]
+                if r == 0 and i == 1:
+                    tile = keep.tile(shape, F32, name="placed0_1", tag="whole1")
+                elif r == LAST:
+                    tile = keep.tile(shape, F32, name="placed_last", align_bytes=64)
+                else:
+                    tile = ring.tile(shape, F32, name="placed", bufs=2)
+                nc.gpsimd.tensor_tensor(tile[:], sines[r][:, cols], weights[r][:, cols], ALU.mult)
+                placed[r].append(tile)
 
         def replace(r):
-            for cols in pieces_of(r):
-                window = pages[r][:].indirect(idx3[:, list_columns(cols)])
-                if r == 0:
-                    nc.vector.tensor_tensor(window, sines[r][:, cols], weights[r][:, cols], ALU.mult)
-                else:
-                    nc.vector.tensor_copy(window, placed[r][:, cols])
+            for cols, tile in zip(pieces_of(r), placed[r]):
+                nc.vector.tensor_copy(pages[r][:].indirect(idx3[:, list_columns(cols)]), tile[:])
 
         x_turned = {}
         for a in range(2):
@@ -271,13 +268,15 @@ def tile_list_veneer_log_grading_kernel(
                     acc[:].rearrange("n (k q u e) -> n k u q e", k=4, u=2, e=2),
                 )
 
+        x_scales = {1: keep.tile([P, 2, BANK], U8, name="x_s1", align_bytes=64)}
+        x_ins = {}
         x_c = {}
         x_s = {}
 
         def turn_back(a, h, banks):
             x_in = keep.tile([P, BANK * PACK], BF16, name="x_in%d_%d" % (a, h), tag="page%d" % (2 * a + h), align_bytes=64)
             codes = keep.tile([P, BANK], U32, name="x_c%d_%d" % (a, h), align_bytes=64)
-            scales = keep.tile([P, BANK], U8, name="x_s%d_%d" % (a, h), align_bytes=64)
+            scales = x_scales[a][:, h, :] if a == 1 else None
             words = x_turned[a, h][:].rearrange("n k u p e -> n (k u p e)").bitcast(F32)
             dst = x_in[:].bitcast(F32)
             for g in range(2):
@@ -295,31 +294,38 @@ def tile_list_veneer_log_grading_kernel(
                         out=codes[:, cols].bitcast(FP8X4), scales=scales[:, cols],
                         in_=x_in[:, PACK * cols.start : PACK * cols.stop],
                     )
-            if a == 0:
-                nc.vector.quantize_mx(out=codes[:].bitcast(FP8X4), scales=scales[:], in_=x_in[:])
+            x_ins[a, h] = x_in
             x_c[a, h] = codes
             x_s[a, h] = scales
 
         quantise_w1(0)
         first_product(0)
         quantise_w1(1)
-        weigh(0)
         sine_of(0)
         first_product(1)
+        early = reuse.tile([P, 2, S], F32, name="weights_early", offset=8192, align_bytes=64)
+        for r in range(2):
+            weights[r] = early[:, r, :]
+            weigh(r)
+        multiply(0)
         for r in range(ROW_TILES):
-            if r + 1 <= LAST:
-                weigh(r + 1)
             if r + 2 <= LAST:
                 first_product(r + 2)
             if r + 1 <= LAST:
                 sine_of(r + 1)
                 multiply(r + 1)
             replace(r)
-
             if r == 0:
                 quantise_w1(2)
+                late = reuse.tile([P, ROW_TILES - 2, S], F32, name="weights_late", offset=10240, align_bytes=64)
+                for k in range(2, ROW_TILES):
+                    weights[k] = late[:, k - 2, :]
+                for k in range(2, 5):
+                    weigh(k)
             if r >= 1:
                 apply_wear(r - 1)
+            if 2 <= r <= 4:
+                weigh(r + 3)
             if r >= 2:
                 add_shift_turned(r - 2)
             if r in (2, 3):
@@ -342,6 +348,10 @@ def tile_list_veneer_log_grading_kernel(
         add_shift_turned(LAST - 1)
         apply_wear(LAST)
         add_shift_turned(LAST)
+        x_scales[0] = keep.tile([P, 2, BANK], U8, name="x_s0", tag="placed_last", align_bytes=64)
+        for h in range(2):
+            x_s[0, h] = x_scales[0][:, h, :]
+            nc.vector.quantize_mx(out=x_c[0, h][:].bitcast(FP8X4), scales=x_s[0, h], in_=x_ins[0, h][:])
         v2_s = gather(keep.tile([P, S], U8, name="v2_s", tag="wear%d" % LAST, align_bytes=64), tab2_s, idx2, WHOLE)
         v2_w = keep.tile([P, 2, S], U32, name="v2_w", tag="page%d" % LAST, align_bytes=64)
         for a in range(2):
@@ -366,7 +376,7 @@ def tile_list_veneer_log_grading_kernel(
 
         for m in range(4):
             top = ring.tile([P, S], F32, name="top", tag="angle")
-            diff = ring.tile([P, S], F32, name="diff", tag="whole", bufs=2)
+            diff = keep.tile([P, S], F32, name="diff%d" % m, tag="whole%d" % (m % 2))
             best = region(m, [P, S], F32, "best%d" % m)
             gather(top, e_sb[m], p2, HALVES)
             for cols in HALVES:

import math
from contextlib import ExitStack

import concourse.mybir as mybir
from concourse.masks import make_identity

FLOPS = 2147483648

F32 = mybir.dt.float32
BF16 = mybir.dt.bfloat16
I32 = mybir.dt.int32
U32 = mybir.dt.uint32
U16 = mybir.dt.uint16
U8 = mybir.dt.uint8
FP8X4 = mybir.dt.float8_e4m3fn_x4
FP4X4 = mybir.dt.float4_e2m1fn_x4
ALU = mybir.AluOpType
ACT = mybir.ActivationFunctionType

P = 128
PACK = 4
K_PASS = P * PACK
T = 2048
S = 512
H = 1024
T2 = 1024
BANK = 512
ROW_TILES = H // P
LAST = ROW_TILES - 1
TWO_PI = 2.0 * math.pi
TURN_OFFSET = 2.0**21 - 0.25
WHOLE = [slice(0, S)]
HALVES = [slice(0, S // 2), slice(S // 2, S)]


def list_columns(cols):
    return slice(cols.start // 16, cols.stop // 16)


def tile_list_veneer_log_grading_kernel(
    tc, tab_words, tab_scales, tab2_words, tab2_scales, w4_words, w4_scales, w1, gain, wgs,
    page0, wear, shift, cv, offs, offs2, offs3, pos1, pos2, out,
):
    nc = tc.nc
    with ExitStack() as ctx:
        keep = ctx.enter_context(tc.tile_pool(name="keep", bufs=1))
        ring = ctx.enter_context(tc.tile_pool(name="ring", bufs=3))
        reuse = ctx.enter_context(tc.tile_pool(name="reuse", bufs=1))
        psum = ctx.enter_context(tc.psum_pool(name="psum", bufs=1))

        def bank(b, name):
            return psum.tile([P, BANK], F32, name=name, tag="bank%d" % b)

        def load_list(src, name):
            tile = keep.tile([P, S // 16], U16, name=name)
            nc.sync.dma_start(tile[:], src)
            return tile

        def load_words(src, a, tile):
            nc.sync.dma_start(tile[:].bitcast(I32), src[a].rearrange("p t i -> p (t i)").bitcast(I32))
            return tile

        def load_scale_rows(src, tile, queue):
            rows = 4 * src.shape[0]
            for q in range(4):
                queue.dma_start(
                    tile[32 * q : 32 * q + rows, :].bitcast(I32), src[:, 4 * q : 4 * q + 4, :].bitcast(I32)
                )

        def gather(tile, window, offsets, pieces):
            for cols in pieces:
                nc.vector.tensor_copy(tile[:, cols], window[:].indirect(offsets[:, list_columns(cols)]))
            return tile

        tab_s = keep.tile([P, T], U8, name="tab_s")
        w_s = keep.tile([P, H], U8, name="w_s", align_bytes=64)
        tab2_s = keep.tile([P, T], U8, name="tab2_s")
        nc.gpsimd.memset(tab_s[:].bitcast(I32), 0)
        load_scale_rows(tab_scales, tab_s, nc.sync)
        nc.vector.memset(tab2_s[:].bitcast(I32), 0)
        ident = keep.tile([P, P], F32, name="ident")
        make_identity(nc, ident[:])
        one = keep.tile([P, 1], F32, name="one")
        half_pi = keep.tile([P, 1], F32, name="half_pi")
        nc.vector.memset(one[:], 1.0)
        nc.vector.tensor_scalar(half_pi[:], one[:], math.pi / 2.0, None, ALU.mult)
        warm = keep.tile([P, 1], F32, name="warm")
        nc.scalar.activation(warm[:], one[:], ACT.Sin)

        w1_rows = w1.rearrange("(p j) c -> p j c", j=PACK)
        w1_parts = [(0, P), (P, K_PASS), (K_PASS, H)]
        w1_raw = []

        def load_w1(part):
            c0, c1 = w1_parts[part]
            tile = keep.tile([P, PACK, c1 - c0], F32, name="w1_raw%d" % part)
            nc.sync.dma_start(tile[:], w1_rows[:, :, c0:c1])
            w1_raw.append(tile)

        def load_rows(src, r, tag):
            tile = keep.tile([P, T2], F32, name="%s_%d" % (tag, r), tag=tag, align_bytes=64)
            nc.sync.dma_start(tile[:], src[P * r : P * (r + 1), :])
            return tile

        idx = load_list(offs, "idx")
        tab_w = [
            load_words(tab_words, 0, keep.tile([P, T], U32, name="tab_w0", tag="words0")),
            load_words(tab_words, 1, reuse.tile([P, T], U32, name="tab_w1", offset=0, align_bytes=64)),
        ]
        load_scale_rows(w4_scales, w_s, nc.sync)
        load_w1(0)
        w4_w = keep.tile([P, 2 * H], U8, name="w4_w", align_bytes=64)
        nc.sync.dma_start(w4_w[:].bitcast(I32), w4_words[0].bitcast(I32))
        load_w1(1)
        wgs_sb = keep.tile([P, S], F32, name="wgs_sb")
        nc.sync.dma_start(wgs_sb[:], wgs)
        gain_sb = keep.tile([P, ROW_TILES], F32, name="gain_sb")
        with nc.allow_non_contiguous_dma(reason="one value to a partition"):
            nc.sync.dma_start(gain_sb[:, 0:PACK], gain[0:K_PASS].rearrange("(c p) -> p c", p=P))
        idx3 = load_list(offs3, "idx3")

        pages = {}
        wears = {}
        shifts = {}

        def load_page(r):
            pages[r] = load_rows(page0, r, "page%d" % r)

        def load_wear(r):
            wears[r] = load_rows(wear, r, "wear%d" % r)

        def load_shift(r):
            shifts[r] = load_rows(shift, r, "rows%d" % (r % 6))

        load_page(0)
        load_page(1)
        load_w1(2)
        gain_hi = keep.tile([P, PACK], F32, name="gain_hi")
        with nc.allow_non_contiguous_dma(reason="one value to a partition"):
            nc.sync.dma_start(gain_hi[:], gain[K_PASS:H].rearrange("(c p) -> p c", p=P))
        for r in range(6):
            load_wear(r)
            load_page(r + 2)
            load_shift(r)
        load_wear(LAST - 1)
        load_wear(LAST)

        v_s = gather(keep.tile([P, S], U8, name="v_s", align_bytes=64), tab_s, idx, WHOLE)
        v_w = [
            gather(keep.tile([P, S], U32, name="v_w0", align_bytes=64), tab_w[0], idx, WHOLE),
            gather(keep.tile([P, S], U32, name="v_w1", align_bytes=64), tab_w[1], idx, HALVES),
        ]

        w1_c = keep.tile([P, H], U32, name="w1_c", align_bytes=64)

        def quantise_w1(part):
            c0, c1 = w1_parts[part]
            width = c1 - c0
            if part == 0:
                grouped = keep.tile([P, width, PACK], BF16, name="w1_bf0", align_bytes=64)
            elif part == 1:
                grouped = reuse.tile([P, width, PACK], BF16, name="w1_bf1", offset=0, align_bytes=64)
            else:
                grouped = reuse.tile([P, width, PACK], BF16, name="w1_bf2", offset=5120, align_bytes=64)
            dst = grouped[:].rearrange("p (c i) j -> p c j i", i=4)
            src = w1_raw[part][:].rearrange("p j (c i) -> p c j i", i=4)
            if part == 1:
                nc.vector.tensor_copy(dst, src)
            else:
                nc.scalar.copy(dst, src)
            cuts = [(c0, 2 * P), (2 * P, c1)] if part == 1 else [(c0, c1)]
            for lo, hi in cuts:
                nc.vector.quantize_mx(
                    out=w1_c[:, lo:hi].bitcast(FP8X4), scales=w_s[4:P, lo:hi],
                    in_=grouped[:, lo - c0 : hi - c0, :].rearrange("p c j -> p (c j)"),
                )

        sines = {}
        weights = {}
        angles = {}
        placed = {}

        def pieces_of(r):
            return HALVES if r == 0 else WHOLE

        def region(r, shape, dtype, name):
            return keep.tile(shape, dtype, name=name, tag="region%d" % (r % 6), align_bytes=64)

        def weigh(r):
            gain_col = gain_sb[:, r : r + 1] if r < PACK else gain_hi[:, r - PACK : r - PACK + 1]
            nc.gpsimd.tensor_scalar(weights[r], wgs_sb[:], gain_col, 0.0, ALU.mult, ALU.add)

        def first_product(r):
            rows = slice(P * r, P * (r + 1))
            turns = region(r, [P, S], U32, "turns%d" % r)
            whole = keep.tile([P, S], F32, name="whole%d" % r, tag="whole%d" % (r % 2))
            angle = ring.tile([P, S], F32, name="angle")
            for i, cols in enumerate(pieces_of(r)):
                y = bank(r % 2 + 6 * i, "y%d_%d" % (r, i))[:, 0 : cols.stop - cols.start]
                nc.tensor.matmul_mx(
                    y, lhsT=w4_w[:, 2 * P * r : 2 * P * (r + 1)].bitcast(FP4X4), lhsT_scale=w_s[:, rows],
                    rhs=v_w[0][:, cols].bitcast(FP8X4), rhs_scale=v_s[:, cols], start=True, stop=False,
                )
                nc.tensor.matmul_mx(
                    y, lhsT=w1_c[:, rows].bitcast(FP8X4), lhsT_scale=w_s[4:P, rows],
                    rhs=v_w[1][:, cols].bitcast(FP8X4), rhs_scale=v_s[4:P, cols], start=False, stop=True,
                )
                nc.scalar.activation(turns[:, cols], y, ACT.Copy, bias=TURN_OFFSET, scale=1.0 / TWO_PI)
                nc.scalar.activation(whole[:, cols], turns[:, cols], ACT.Copy, bias=-TURN_OFFSET, scale=1.0)
                nc.vector.scalar_tensor_tensor(angle[:, cols], whole[:, cols], -TWO_PI, y, ALU.mult, ALU.add)
            angles[r] = angle

        def sine_of(r):
            angle = angles[r]
            sine = region(r - 1, [P, S], F32, "sine%d" % r)
            for cols in pieces_of(r):
                nc.scalar.activation(angle[:, cols], angle[:, cols], ACT.Abs)
                nc.scalar.activation(sine[:, cols], angle[:, cols], ACT.Sin, bias=half_pi[:], scale=-1.0)
            sines[r] = sine

        def multiply(r):
            placed[r] = []
            for i, cols in enumerate(pieces_of(r)):
                shape = [P, cols.stop - cols.start]
                if r == 0 and i == 1:
                    tile = keep.tile(shape, F32, name="placed0_1", tag="whole1")
                elif r == LAST:
                    tile = keep.tile(shape, F32, name="placed_last", align_bytes=64)
                else:
                    tile = ring.tile(shape, F32, name="placed", bufs=2)
                nc.gpsimd.tensor_tensor(tile[:], sines[r][:, cols], weights[r][:, cols], ALU.mult)
                placed[r].append(tile)

        def replace(r):
            for cols, tile in zip(pieces_of(r), placed[r]):
                nc.vector.tensor_copy(pages[r][:].indirect(idx3[:, list_columns(cols)]), tile[:])

        x_turned = {}
        for a in range(2):
            for h in range(2):
                x_turned[a, h] = keep.tile([P, 4, 2, P, 2], BF16, name="x_turned%d_%d" % (a, h))

        worns = {}

        def apply_wear(r):
            worns[r] = region(r, [P, T2], F32, "worn%d" % r)
            if r < LAST:
                nc.gpsimd.tensor_tensor(worns[r][:], pages[r][:], wears[r][:], ALU.mult)
            else:
                for h in range(2):
                    cols = slice(BANK * h, BANK * (h + 1))
                    nc.vector.tensor_tensor(worns[r][:, cols], pages[r][:, cols], wears[r][:, cols], ALU.mult)

        def add_shift_turned(r):
            worn = worns[r]
            c = r % PACK
            for h in range(2):
                acc = bank(2 + 2 * (r % 2) + h, "xt%d_%d" % (r, h))
                for which, src in enumerate((shifts[r], worn)):
                    for k in range(4):
                        n0 = BANK * h + P * k
                        nc.tensor.matmul(
                            acc[:, P * k : P * (k + 1)], lhsT=src[:, n0 : n0 + P], rhs=ident[:],
                            is_transpose=True, start=(which == 0 and k == 0), stop=(which == 1 and k == 3),
                        )
                nc.scalar.copy(
                    x_turned[r // PACK, h][:, :, :, 32 * c : 32 * (c + 1), :],
                    acc[:].rearrange("n (k q u e) -> n k u q e", k=4, u=2, e=2),
                )

        x_scales = {1: keep.tile([P, 2, BANK], U8, name="x_s1", align_bytes=64)}
        x_ins = {}
        x_c = {}
        x_s = {}

        def turn_back(a, h, banks):
            x_in = keep.tile([P, BANK * PACK], BF16, name="x_in%d_%d" % (a, h), tag="page%d" % (2 * a + h), align_bytes=64)
            codes = keep.tile([P, BANK], U32, name="x_c%d_%d" % (a, h), align_bytes=64)
            scales = x_scales[a][:, h, :] if a == 1 else None
            words = x_turned[a, h][:].rearrange("n k u p e -> n (k u p e)").bitcast(F32)
            dst = x_in[:].bitcast(F32)
            for g in range(2):
                acc = bank(banks[g], "xw%d_%d_%d" % (a, h, g))
                for i in range(4):
                    w0 = BANK * g + P * i
                    nc.tensor.transpose(acc[:, P * i : P * (i + 1)], words[:, w0 : w0 + P], ident[:])
                nc.scalar.copy(
                    dst[:, BANK * g : BANK * (g + 1)].rearrange("p (k n u) -> p k n u", k=2, u=2),
                    acc[:].rearrange("p (k u n) -> p k n u", k=2, u=2),
                )
                if a == 1:
                    cols = HALVES[g]
                    nc.vector.quantize_mx(
                        out=codes[:, cols].bitcast(FP8X4), scales=scales[:, cols],
                        in_=x_in[:, PACK * cols.start : PACK * cols.stop],
                    )
            x_ins[a, h] = x_in
            x_c[a, h] = codes
            x_s[a, h] = scales

        quantise_w1(0)
        first_product(0)
        quantise_w1(1)
        sine_of(0)
        first_product(1)
        early = reuse.tile([P, 2, S], F32, name="weights_early", offset=8192, align_bytes=64)
        for r in range(2):
            weights[r] = early[:, r, :]
            weigh(r)
        multiply(0)
        for r in range(ROW_TILES):
            if r + 2 <= LAST:
                first_product(r + 2)
            if r + 1 <= LAST:
                sine_of(r + 1)
                multiply(r + 1)
            replace(r)
            if r == 0:
                quantise_w1(2)
                late = reuse.tile([P, ROW_TILES - 2, S], F32, name="weights_late", offset=10240, align_bytes=64)
                for k in range(2, ROW_TILES):
                    weights[k] = late[:, k - 2, :]
                for k in range(2, 5):
                    weigh(k)
            if r >= 1:
                apply_wear(r - 1)
            if 2 <= r <= 4:
                weigh(r + 3)
            if r >= 2:
                add_shift_turned(r - 2)
            if r in (2, 3):
                load_shift(LAST - 3 + r)
            if r == 2:
                idx2 = load_list(offs2, "idx2")
                load_scale_rows(tab2_scales, tab2_s, nc.sync)
                tab2_w = [
                    load_words(tab2_words, a, keep.tile([P, T], U32, name="tab2_w%d" % a, tag="words%d" % a))
                    for a in range(2)
                ]
                cv_sb = keep.tile([P, PACK], F32, name="cv_sb")
                with nc.allow_non_contiguous_dma(reason="one value to a partition"):
                    nc.sync.dma_start(cv_sb[:], cv.rearrange("(c p) -> p c", p=P))
                p1 = load_list(pos1, "p1")
                p2 = load_list(pos2, "p2")
            if r == PACK + 1:
                turn_back(0, 0, (6, 7))
                turn_back(0, 1, (6, 7))
        add_shift_turned(LAST - 1)
        apply_wear(LAST)
        add_shift_turned(LAST)
        x_scales[0] = keep.tile([P, 2, BANK], U8, name="x_s0", tag="placed_last", align_bytes=64)
        for h in range(2):
            x_s[0, h] = x_scales[0][:, h, :]
            nc.vector.quantize_mx(out=x_c[0, h][:].bitcast(FP8X4), scales=x_s[0, h], in_=x_ins[0, h][:])
        v2_s = gather(keep.tile([P, S], U8, name="v2_s", tag="wear%d" % LAST, align_bytes=64), tab2_s, idx2, WHOLE)
        v2_w = keep.tile([P, 2, S], U32, name="v2_w", tag="page%d" % LAST, align_bytes=64)
        for a in range(2):
            nc.vector.tensor_copy(v2_w[:, a, :], tab2_w[a][:].indirect(idx2[:]))
        turn_back(1, 0, (0, 1))
        turn_back(1, 1, (6, 7))

        score_banks = ((0, 6), (1, 7), (0, 6), (1, 7))
        e_sb = [keep.tile([P, T2], F32, name="e%d" % m, tag="rows%d" % (2 + m), align_bytes=64) for m in range(4)]
        for m in range(4):
            grades = slice(P * m, P * (m + 1))
            for h in range(2):
                acc = bank(score_banks[m][h], "e%d_%d" % (m, h))
                for a, cols in ((0, WHOLE[0]), (1, HALVES[0]), (1, HALVES[1])):
                    nc.tensor.matmul_mx(
                        acc[:, cols], lhsT=v2_w[:, a, grades].bitcast(FP8X4), lhsT_scale=v2_s[4 * a : P, grades],
                        rhs=x_c[a, h][:, cols].bitcast(FP8X4), rhs_scale=x_s[a, h][:, cols],
                        start=(a == 0), stop=(cols.stop == S and a == 1),
                    )
                nc.scalar.copy(e_sb[m][:, BANK * h : BANK * (h + 1)], acc[:])


        for m in range(4):
            top = ring.tile([P, S], F32, name="top", tag="angle")
            diff = keep.tile([P, S], F32, name="diff%d" % m, tag="whole%d" % (m % 2))
            best = region(m, [P, S], F32, "best%d" % m)
            gather(top, e_sb[m], p2, HALVES)
            for cols in HALVES:
                picked = e_sb[m][:].indirect(p1[:, list_columns(cols)])
                nc.vector.tensor_tensor(diff[:, cols], picked, top[:, cols], ALU.subtract)
            for cols in HALVES:
                nc.vector.scalar_tensor_tensor(
                    best[:, cols], top[:, cols], cv_sb[:, m : m + 1], diff[:, cols], ALU.mult, ALU.max
                )
            nc.sync.dma_start(out[P * m : P * (m + 1), :], best[:])
